import numpy as np
import ml_dtypes


def mxq(x, axis, fmt="e4m3"):
    dtype, down = {"e4m3": (ml_dtypes.float8_e4m3fn, 7), "e5m2": (ml_dtypes.float8_e5m2, 14)}[fmt]
    v = np.moveaxis(np.asarray(x, np.float32).astype(ml_dtypes.bfloat16).astype(np.float64), axis, -1)
    blocks = v.reshape(v.shape[:-1] + (-1, 32))
    amax = np.abs(blocks).max(-1, keepdims=True)
    byte = np.maximum(np.where(amax > 0, np.frexp(amax)[1] - 1 + 127, 0) - down, 1)
    scale = np.exp2(byte - 127.0)
    codes = (blocks / scale).astype(np.float32).astype(dtype).astype(np.float64)
    return np.moveaxis((codes * scale).reshape(v.shape), -1, axis)


WIDE = False


def mx_kscale(k):
    if not WIDE:
        return np.ones(k)
    levels = np.array([10, -10, 5, -5, 0])
    if k % 512:
        return np.exp2(np.random.permutation(np.resize(levels, k // 32))).repeat(32)
    a = np.empty((k // 512, 16))
    for p in range(k // 512):
        a[p, :8] = np.random.permutation(np.resize(levels, 8))
        for g in range(8):
            far = levels[np.abs(levels - a[p, g]) >= 10]
            a[p, g + 8] = far[np.random.randint(len(far))]
    return np.exp2(a.ravel()).repeat(32)


def f64(x):
    return np.asarray(x).astype(np.float64)


def striped(idx):
    return np.tile(idx.reshape(-1, 16).T, (8, 1)).astype(np.uint16)


def unstriped(offs):
    return offs[:16].T.reshape(-1).astype(np.int64)


def pack_weight(w):
    k, n = w.shape
    w = f64(np.asarray(w, np.float32).astype(ml_dtypes.bfloat16)).reshape(k // 32, 32, n)
    amax = np.abs(w).max(1)
    byte = np.clip(np.where(amax > 0, np.frexp(amax)[1] - 1 + 127 - 7, 1), 1, 254)
    scaled = (w * np.exp2(127.0 - byte)[:, None, :]).reshape(k, n).astype(np.float32)
    words = np.ascontiguousarray(scaled.reshape(k // 512, 128, 4, n).transpose(0, 1, 3, 2)).astype(ml_dtypes.float8_e4m3fn).view(np.uint8)
    return words, np.ascontiguousarray(byte.astype(np.uint8).reshape(k // 512, 16, n))


def unpack_weight(words, scales):
    g, p, n, _ = words.shape
    vals = np.ascontiguousarray(words).view(ml_dtypes.float8_e4m3fn).astype(np.float64) * np.repeat(np.exp2(scales.astype(np.float64) - 127.0), 8, axis=1)[..., None]
    return vals.transpose(0, 1, 3, 2).reshape(g * 512, n)


def gelu(v):
    return 0.5 * v * (1.0 + np.tanh(np.sqrt(2.0 / np.pi) * (v + 0.044715 * v**3)))


K, T, E, C, N = 1024, 640, 4, 128, 128


def by_expert(wq, xq):
    return np.concatenate([wq[e].T @ xq[:, e * C:(e + 1) * C] for e in range(E)], axis=1)


def setup_inputs():
    n = np.random.standard_normal
    s = mx_kscale(K)[:, None]
    packed = [pack_weight(m) for m in n((E, K, N)) / np.sqrt(K) / s[None]]
    return {
        "xT": (n((K, T)) * s).astype(np.float32),
        "w_words": np.stack([m[0] for m in packed]),
        "w_scales": np.stack([m[1] for m in packed]),
        "b": (0.3 * n((N, E))).astype(np.float32),
        "gate": np.tile(np.random.uniform(0.2, 1.0, E * C), (N, 1)).astype(np.float32),
        "offs": striped(np.random.permutation(T)[:E * C]),
        "dst": striped(np.random.permutation(T)[:E * C]),
    }


def reference(xT, w_words, w_scales, b, gate, offs, dst):
    idx = unstriped(offs)
    w = np.stack([unpack_weight(w_words[e], w_scales[e]) for e in range(E)])
    xq = mxq(f64(xT)[:, idx], 0, "e4m3")
    y = by_expert(w, xq)
    y = gelu(y + np.repeat(f64(b), C, axis=1))
    out = np.zeros((N, T))
    out[:, unstriped(dst)] = f64(gate) * y
    return out

@@ -1,0 +1,152 @@
+from contextlib import ExitStack
+
+import concourse.mybir as mybir
+
+K, T, E, C, N = 1024, 640, 4, 128, 128
+P = 128
+S = E * C
+FLOPS = 2 * S * K * N
+
+F32 = mybir.dt.float32
+BF16 = mybir.dt.bfloat16
+U32 = mybir.dt.uint32
+I32 = mybir.dt.int32
+U16 = mybir.dt.uint16
+U8 = mybir.dt.uint8
+FP8X4 = mybir.dt.float8_e4m3fn_x4
+GELU = mybir.ActivationFunctionType.Gelu_apprx_tanh
+COPY = mybir.ActivationFunctionType.Copy
+MULT = mybir.AluOpType.mult
+
+CHUNKS = (
+    (0, 0, 256, 128, (256,)),
+    (0, 256, 384, 160, (256, 128)),
+    (1, 0, 256, 112, (256,)),
+    (1, 256, 256, 112, (256,)),
+    (1, 512, 128, 64, (128,)),
+)
+
+
+def tile_moe_two_lin_gelu_kernel(tc, xT, w_words, w_scales, b, gate, offs, dst, out):
+    nc = tc.nc
+    with ExitStack() as ctx:
+        keep = ctx.enter_context(tc.tile_pool(name="keep", bufs=1))
+        psum = ctx.enter_context(tc.psum_pool(name="psum", bufs=1))
+
+        offs_t = keep.tile([P, S // 16], U16, name="offs_t")
+        dst_t = keep.tile([P, S // 16], U16, name="dst_t")
+        nc.sync.dma_start(offs_t[:], offs)
+        nc.sync.dma_start(dst_t[:], dst)
+        b_t = keep.tile([P, E], F32, name="b_t")
+        nc.sync.dma_start(b_t[:], b)
+
+        raws = []
+        for i, (a, t0, n, nv, qs) in enumerate(CHUNKS):
+            raw = keep.tile([P, 4, n], F32, name=f"raw{i}")
+            nc.sync.dma_start(
+                raw[:],
+                xT[512 * a : 512 * (a + 1), t0 : t0 + n].rearrange("(p j) t -> p j t", j=4),
+            )
+            raws.append(raw)
+
+        ws = keep.tile([P, 2 * E, N], U8, name="ws", align_bytes=64)
+        nc.vector.memset(ws[:].rearrange("p g n -> p (g n)").bitcast(I32), 0)
+        xs = keep.tile([P, T], U8, name="xs", align_bytes=64)
+        nc.gpsimd.memset(xs[:], 0)
+        o_t = keep.tile([P, T], F32, name="o_t")
+        nc.vector.memset(o_t[:], 0.0)
+        warm = keep.tile([P, 1], F32, name="warm")
+        nc.vector.memset(warm[:], 0.0)
+        nc.scalar.activation(warm[:], warm[:], GELU)
+
+        for q in range(4):
+            nc.sync.dma_start(
+                ws[32 * q : 32 * q + 4, :, :].bitcast(I32),
+                w_scales[:, :, 4 * q : 4 * q + 4, :].rearrange("e a q n -> q (e a) n").bitcast(I32),
+            )
+        ww = []
+        for h in range(2):
+            w_t = keep.tile([P, 4, N], I32, name=f"w{h}", align_bytes=64)
+            nc.sync.dma_start(
+                w_t[:],
+                w_words[2 * h : 2 * h + 2].rearrange("e a p n r -> p (e a) (n r)").bitcast(I32),
+            )
+            ww.append(w_t)
+        gate_t = keep.tile([P, S], F32, name="gate_t")
+        nc.sync.dma_start(gate_t[:], gate)
+
+        xw = [keep.tile([P, T], U32, name=f"xw{a}", align_bytes=64) for a in range(2)]
+        gw = [[keep.tile([P, 2 * C], U32, name=f"gw{a}{h}", align_bytes=64) for h in range(2)] for a in range(2)]
+        gb = [keep.tile([P, 2 * C], U8, name=f"gb{h}", align_bytes=64) for h in range(2)]
+
+        def cast(i):
+            a, t0, n, nv, qs = CHUNKS[i]
+            g = keep.tile([P, n, 4], BF16, name=f"g{i}", align_bytes=64)
+            src = raws[i][:].rearrange("p j t -> p t j")
+            nc.vector.tensor_copy(g[:, 0:nv, :], src[:, 0:nv, :])
+            nc.scalar.activation(g[:, nv:n, :], src[:, nv:n, :], COPY)
+            return g
+
+        def quantize(i, g):
+            a, t0, n, nv, qs = CHUNKS[i]
+            s = 0
+            for w in qs:
+                cols = slice(t0 + s, t0 + s + w)
+                nc.vector.quantize_mx(
+                    out=xw[a][:, cols].bitcast(FP8X4),
+                    scales=xs[4 * a : P, cols],
+                    in_=g[:, s : s + w, :].rearrange("p t j -> p (t j)"),
+                )
+                s += w
+
+        def list_of(tile, h):
+            return tile[:, 16 * h : 16 * h + 16]
+
+        def gather_words(a, h):
+            nc.vector.tensor_copy(gw[a][h][:], xw[a][:].indirect(list_of(offs_t, h)))
+
+        def gather_bytes(h):
+            nc.vector.tensor_copy(gb[h][:], xs[:].indirect(list_of(offs_t, h)))
+
+        g0 = cast(0)
+        quantize(0, g0)
+        g1 = cast(1)
+        quantize(1, g1)
+        g2 = cast(2)
+        gather_words(0, 0)
+        quantize(2, g2)
+        g3 = cast(3)
+        gather_words(0, 1)
+        quantize(3, g3)
+        g4 = cast(4)
+        quantize(4, g4)
+
+        ys = []
+        for h in range(2):
+            gather_bytes(h)
+            gather_words(1, h)
+            for e in (2 * h, 2 * h + 1):
+                c = slice((e - 2 * h) * C, (e - 2 * h + 1) * C)
+                ps = psum.tile([P, C], F32, name=f"ps{e}")
+                for a in range(2):
+                    nc.tensor.matmul_mx(
+                        out=ps[:],
+                        lhsT=ww[h][:, 2 * (e - 2 * h) + a, :].bitcast(FP8X4),
+                        lhsT_scale=ws[:, 2 * e + a, :],
+                        rhs=gw[a][h][:, c].bitcast(FP8X4),
+                        rhs_scale=gb[h][4 * a : P, c],
+                        start=(a == 0),
+                        stop=(a == 1),
+                    )
+                y = keep.tile([P, C], F32, name=f"y{e}")
+                nc.scalar.activation(y[:], ps[:], GELU, bias=b_t[:, e : e + 1])
+                ys.append(y)
+
+        for e in range(E):
+            nc.vector.tensor_tensor(
+                o_t[:].indirect(dst_t[:, 8 * e : 8 * e + 8]),
+                ys[e][:],
+                gate_t[:, e * C : (e + 1) * C],
+                MULT,
+            )
+        nc.sync.dma_start(out, o_t[:])

@@ -20,9 +20,9 @@ MULT = mybir.AluOpType.mult
 
 CHUNKS = (
     (0, 0, 256, 128, (256,)),
-    (0, 256, 384, 160, (256, 128)),
-    (1, 0, 256, 112, (256,)),
-    (1, 256, 256, 112, (256,)),
+    (0, 256, 384, 96, (256, 128)),
+    (1, 0, 256, 32, (256,)),
+    (1, 256, 256, 64, (256,)),
     (1, 512, 128, 64, (128,)),
 )
 
@@ -35,10 +35,7 @@ def tile_moe_two_lin_gelu_kernel(tc, xT, w_words, w_scales, b, gate, offs, dst, 
 
         offs_t = keep.tile([P, S // 16], U16, name="offs_t")
         dst_t = keep.tile([P, S // 16], U16, name="dst_t")
-        nc.sync.dma_start(offs_t[:], offs)
-        nc.sync.dma_start(dst_t[:], dst)
         b_t = keep.tile([P, E], F32, name="b_t")
-        nc.sync.dma_start(b_t[:], b)
 
         raws = []
         for i, (a, t0, n, nv, qs) in enumerate(CHUNKS):
@@ -48,6 +45,8 @@ def tile_moe_two_lin_gelu_kernel(tc, xT, w_words, w_scales, b, gate, offs, dst, 
                 xT[512 * a : 512 * (a + 1), t0 : t0 + n].rearrange("(p j) t -> p j t", j=4),
             )
             raws.append(raw)
+            if i == 0:
+                nc.sync.dma_start(offs_t[:], offs)
 
         ws = keep.tile([P, 2 * E, N], U8, name="ws", align_bytes=64)
         nc.vector.memset(ws[:].rearrange("p g n -> p (g n)").bitcast(I32), 0)
@@ -72,8 +71,10 @@ def tile_moe_two_lin_gelu_kernel(tc, xT, w_words, w_scales, b, gate, offs, dst, 
                 w_words[2 * h : 2 * h + 2].rearrange("e a p n r -> p (e a) (n r)").bitcast(I32),
             )
             ww.append(w_t)
+        nc.sync.dma_start(b_t[:], b)
         gate_t = keep.tile([P, S], F32, name="gate_t")
         nc.sync.dma_start(gate_t[:], gate)
+        nc.sync.dma_start(dst_t[:], dst)
 
         xw = [keep.tile([P, T], U32, name=f"xw{a}", align_bytes=64) for a in range(2)]
         gw = [[keep.tile([P, 2 * C], U32, name=f"gw{a}{h}", align_bytes=64) for h in range(2)] for a in range(2)]
@@ -123,6 +124,8 @@ def tile_moe_two_lin_gelu_kernel(tc, xT, w_words, w_scales, b, gate, offs, dst, 
 
         ys = []
         for h in range(2):
+            y = keep.tile([P, 2 * C], F32, name=f"y{h}")
+            ys.append(y)
             gather_bytes(h)
             gather_words(1, h)
             for e in (2 * h, 2 * h + 1):
@@ -138,15 +141,13 @@ def tile_moe_two_lin_gelu_kernel(tc, xT, w_words, w_scales, b, gate, offs, dst, 
                         start=(a == 0),
                         stop=(a == 1),
                     )
-                y = keep.tile([P, C], F32, name=f"y{e}")
-                nc.scalar.activation(y[:], ps[:], GELU, bias=b_t[:, e : e + 1])
-                ys.append(y)
+                nc.scalar.activation(y[:, c], ps[:], GELU, bias=b_t[:, e : e + 1])
 
-        for e in range(E):
+        for h in range(2):
             nc.vector.tensor_tensor(
-                o_t[:].indirect(dst_t[:, 8 * e : 8 * e + 8]),
-                ys[e][:],
-                gate_t[:, e * C : (e + 1) * C],
+                o_t[:].indirect(list_of(dst_t, h)),
+                ys[h][:],
+                gate_t[:, 2 * h * C : 2 * (h + 1) * C],
                 MULT,
             )
         nc.sync.dma_start(out, o_t[:])

@@ -19,11 +19,10 @@ COPY = mybir.ActivationFunctionType.Copy
 MULT = mybir.AluOpType.mult
 
 CHUNKS = (
-    (0, 0, 256, 128, (256,)),
-    (0, 256, 384, 96, (256, 128)),
-    (1, 0, 256, 32, (256,)),
-    (1, 256, 256, 64, (256,)),
-    (1, 512, 128, 64, (128,)),
+    (0, 0, 640, 0, (512, 128)),
+    (1, 0, 256, 0, (256,)),
+    (1, 256, 256, 96, (256,)),
+    (1, 512, 128, 80, (128,)),
 )
 
 
@@ -50,6 +49,11 @@ def tile_moe_two_lin_gelu_kernel(tc, xT, w_words, w_scales, b, gate, offs, dst, 
 
         ws = keep.tile([P, 2 * E, N], U8, name="ws", align_bytes=64)
         nc.vector.memset(ws[:].rearrange("p g n -> p (g n)").bitcast(I32), 0)
+        for q in range(4):
+            nc.scalar.dma_start(
+                ws[32 * q : 32 * q + 4, :, :].bitcast(I32),
+                w_scales[:, :, 4 * q : 4 * q + 4, :].rearrange("e a q n -> q (e a) n").bitcast(I32),
+            )
         xs = keep.tile([P, T], U8, name="xs", align_bytes=64)
         nc.gpsimd.memset(xs[:], 0)
         o_t = keep.tile([P, T], F32, name="o_t")
@@ -58,11 +62,6 @@ def tile_moe_two_lin_gelu_kernel(tc, xT, w_words, w_scales, b, gate, offs, dst, 
         nc.vector.memset(warm[:], 0.0)
         nc.scalar.activation(warm[:], warm[:], GELU)
 
-        for q in range(4):
-            nc.sync.dma_start(
-                ws[32 * q : 32 * q + 4, :, :].bitcast(I32),
-                w_scales[:, :, 4 * q : 4 * q + 4, :].rearrange("e a q n -> q (e a) n").bitcast(I32),
-            )
         ww = []
         for h in range(2):
             w_t = keep.tile([P, 4, N], I32, name=f"w{h}", align_bytes=64)
@@ -84,7 +83,8 @@ def tile_moe_two_lin_gelu_kernel(tc, xT, w_words, w_scales, b, gate, offs, dst, 
             a, t0, n, nv, qs = CHUNKS[i]
             g = keep.tile([P, n, 4], BF16, name=f"g{i}", align_bytes=64)
             src = raws[i][:].rearrange("p j t -> p t j")
-            nc.vector.tensor_copy(g[:, 0:nv, :], src[:, 0:nv, :])
+            if nv > 0:
+                nc.vector.tensor_copy(g[:, 0:nv, :], src[:, 0:nv, :])
             nc.scalar.activation(g[:, nv:n, :], src[:, nv:n, :], COPY)
             return g
 
@@ -109,18 +109,27 @@ def tile_moe_two_lin_gelu_kernel(tc, xT, w_words, w_scales, b, gate, offs, dst, 
         def gather_bytes(h):
             nc.vector.tensor_copy(gb[h][:], xs[:].indirect(list_of(offs_t, h)))
 
-        g0 = cast(0)
-        quantize(0, g0)
+        g0 = []
+        for t0, n, nv in ((0, 512, 336), (512, 128, 80)):
+            g = keep.tile([P, n, 4], BF16, name=f"g0{t0}", align_bytes=64)
+            src = raws[0][:].rearrange("p j t -> p t j")
+            nc.vector.tensor_copy(g[:, 0:nv, :], src[:, t0 : t0 + nv, :])
+            nc.scalar.activation(g[:, nv:n, :], src[:, t0 + nv : t0 + n, :], COPY)
+            g0.append((t0, n, g))
+        for t0, n, g in g0:
+            nc.vector.quantize_mx(
+                out=xw[0][:, t0 : t0 + n].bitcast(FP8X4),
+                scales=xs[:, t0 : t0 + n],
+                in_=g[:].rearrange("p t j -> p (t j)"),
+            )
         g1 = cast(1)
+        gather_words(0, 0)
+        gather_words(0, 1)
         quantize(1, g1)
         g2 = cast(2)
-        gather_words(0, 0)
-        quantize(2, g2)
         g3 = cast(3)
-        gather_words(0, 1)
+        quantize(2, g2)
         quantize(3, g3)
-        g4 = cast(4)
-        quantize(4, g4)
 
         ys = []
         for h in range(2):

from contextlib import ExitStack

import concourse.mybir as mybir

K, T, E, C, N = 1024, 640, 4, 128, 128
P = 128
S = E * C
FLOPS = 2 * S * K * N

F32 = mybir.dt.float32
BF16 = mybir.dt.bfloat16
U32 = mybir.dt.uint32
I32 = mybir.dt.int32
U16 = mybir.dt.uint16
U8 = mybir.dt.uint8
FP8X4 = mybir.dt.float8_e4m3fn_x4
GELU = mybir.ActivationFunctionType.Gelu_apprx_tanh
COPY = mybir.ActivationFunctionType.Copy
MULT = mybir.AluOpType.mult

CHUNKS = (
    (0, 0, 640, 0, (512, 128)),
    (1, 0, 256, 0, (256,)),
    (1, 256, 256, 96, (256,)),
    (1, 512, 128, 80, (128,)),
)


def tile_moe_two_lin_gelu_kernel(tc, xT, w_words, w_scales, b, gate, offs, dst, out):
    nc = tc.nc
    with ExitStack() as ctx:
        keep = ctx.enter_context(tc.tile_pool(name="keep", bufs=1))
        psum = ctx.enter_context(tc.psum_pool(name="psum", bufs=1))

        offs_t = keep.tile([P, S // 16], U16, name="offs_t")
        dst_t = keep.tile([P, S // 16], U16, name="dst_t")
        b_t = keep.tile([P, E], F32, name="b_t")

        raws = []
        for i, (a, t0, n, nv, qs) in enumerate(CHUNKS):
            raw = keep.tile([P, 4, n], F32, name=f"raw{i}")
            nc.sync.dma_start(
                raw[:],
                xT[512 * a : 512 * (a + 1), t0 : t0 + n].rearrange("(p j) t -> p j t", j=4),
            )
            raws.append(raw)
            if i == 0:
                nc.sync.dma_start(offs_t[:], offs)

        ws = keep.tile([P, 2 * E, N], U8, name="ws", align_bytes=64)
        nc.vector.memset(ws[:].rearrange("p g n -> p (g n)").bitcast(I32), 0)
        for q in range(4):
            nc.scalar.dma_start(
                ws[32 * q : 32 * q + 4, :, :].bitcast(I32),
                w_scales[:, :, 4 * q : 4 * q + 4, :].rearrange("e a q n -> q (e a) n").bitcast(I32),
            )
        xs = keep.tile([P, T], U8, name="xs", align_bytes=64)
        nc.gpsimd.memset(xs[:], 0)
        o_t = keep.tile([P, T], F32, name="o_t")
        nc.vector.memset(o_t[:], 0.0)
        warm = keep.tile([P, 1], F32, name="warm")
        nc.vector.memset(warm[:], 0.0)
        nc.scalar.activation(warm[:], warm[:], GELU)

        ww = []
        for h in range(2):
            w_t = keep.tile([P, 4, N], I32, name=f"w{h}", align_bytes=64)
            nc.sync.dma_start(
                w_t[:],
                w_words[2 * h : 2 * h + 2].rearrange("e a p n r -> p (e a) (n r)").bitcast(I32),
            )
            ww.append(w_t)
        nc.sync.dma_start(b_t[:], b)
        gate_t = keep.tile([P, S], F32, name="gate_t")
        nc.sync.dma_start(gate_t[:], gate)
        nc.sync.dma_start(dst_t[:], dst)

        xw = [keep.tile([P, T], U32, name=f"xw{a}", align_bytes=64) for a in range(2)]
        gw = [[keep.tile([P, 2 * C], U32, name=f"gw{a}{h}", align_bytes=64) for h in range(2)] for a in range(2)]
        gb = [keep.tile([P, 2 * C], U8, name=f"gb{h}", align_bytes=64) for h in range(2)]

        def cast(i):
            a, t0, n, nv, qs = CHUNKS[i]
            g = keep.tile([P, n, 4], BF16, name=f"g{i}", align_bytes=64)
            src = raws[i][:].rearrange("p j t -> p t j")
            if nv > 0:
                nc.vector.tensor_copy(g[:, 0:nv, :], src[:, 0:nv, :])
            nc.scalar.activation(g[:, nv:n, :], src[:, nv:n, :], COPY)
            return g

        def quantize(i, g):
            a, t0, n, nv, qs = CHUNKS[i]
            s = 0
            for w in qs:
                cols = slice(t0 + s, t0 + s + w)
                nc.vector.quantize_mx(
                    out=xw[a][:, cols].bitcast(FP8X4),
                    scales=xs[4 * a : P, cols],
                    in_=g[:, s : s + w, :].rearrange("p t j -> p (t j)"),
                )
                s += w

        def list_of(tile, h):
            return tile[:, 16 * h : 16 * h + 16]

        def gather_words(a, h):
            nc.vector.tensor_copy(gw[a][h][:], xw[a][:].indirect(list_of(offs_t, h)))

        def gather_bytes(h):
            nc.vector.tensor_copy(gb[h][:], xs[:].indirect(list_of(offs_t, h)))

        g0 = []
        for t0, n, nv in ((0, 512, 336), (512, 128, 80)):
            g = keep.tile([P, n, 4], BF16, name=f"g0{t0}", align_bytes=64)
            src = raws[0][:].rearrange("p j t -> p t j")
            nc.vector.tensor_copy(g[:, 0:nv, :], src[:, t0 : t0 + nv, :])
            nc.scalar.activation(g[:, nv:n, :], src[:, t0 + nv : t0 + n, :], COPY)
            g0.append((t0, n, g))
        for t0, n, g in g0:
            nc.vector.quantize_mx(
                out=xw[0][:, t0 : t0 + n].bitcast(FP8X4),
                scales=xs[:, t0 : t0 + n],
                in_=g[:].rearrange("p t j -> p (t j)"),
            )
        g1 = cast(1)
        gather_words(0, 0)
        gather_words(0, 1)
        quantize(1, g1)
        g2 = cast(2)
        g3 = cast(3)
        quantize(2, g2)
        quantize(3, g3)

        ys = []
        for h in range(2):
            y = keep.tile([P, 2 * C], F32, name=f"y{h}")
            ys.append(y)
            gather_bytes(h)
            gather_words(1, h)
            for e in (2 * h, 2 * h + 1):
                c = slice((e - 2 * h) * C, (e - 2 * h + 1) * C)
                ps = psum.tile([P, C], F32, name=f"ps{e}")
                for a in range(2):
                    nc.tensor.matmul_mx(
                        out=ps[:],
                        lhsT=ww[h][:, 2 * (e - 2 * h) + a, :].bitcast(FP8X4),
                        lhsT_scale=ws[:, 2 * e + a, :],
                        rhs=gw[a][h][:, c].bitcast(FP8X4),
                        rhs_scale=gb[h][4 * a : P, c],
                        start=(a == 0),
                        stop=(a == 1),
                    )
                nc.scalar.activation(y[:, c], ps[:], GELU, bias=b_t[:, e : e + 1])

        for h in range(2):
            nc.vector.tensor_tensor(
                o_t[:].indirect(list_of(dst_t, h)),
                ys[h][:],
                gate_t[:, 2 * h * C : 2 * (h + 1) * C],
                MULT,
            )
        nc.sync.dma_start(out, o_t[:])
